import numpy as np
CORES = [96,97,98,99,100,101,102,103,112,113,114,115,116,117,118,119]
N = 16
def setup_inputs(rng):
    return {"x1": rng.standard_normal((N, 128, 16), dtype=np.float32), "x2": rng.standard_normal((N, 128, 128), dtype=np.float32)}
def reference(x1, x2):
    out = []
    s = x1.sum(axis=0, dtype=np.float64).astype(x1.dtype)
    out.append(np.broadcast_to(s, (N,) + s.shape))
    g = np.concatenate(list(x2), axis=1)
    out.append(np.broadcast_to(g, (N,) + g.shape))
    return {"y1": out[0], "y2": out[1]}

@@ -1,0 +1,87 @@
+from concourse.bass import DstId, RemoteDMATransfer
+
+SCRATCH = {
+    "land": ("sbuf", [128, 2048], "float32"),
+    "g1": ("dram", [16, 128, 16], "float32"),
+    "res": ("dram", [128, 16], "float32"),
+}
+SEMAPHORES = ["ld1", "ld2", "xarr", "arrA", "arrB", "a1", "r1", "sent", "st1", "st2", "sty"]
+
+ROOT_K = 0
+
+
+def rank_program(g, core, T, topo):
+    rank = T.rank_of(core)
+    if rank is None:
+        return
+    S = T.sem
+    cores = T.cores
+    half, k = divmod(rank, 8)
+    partner_rank = (1 - half) * 8 + k
+    partner = cores[partner_rank]
+    peers = [cores[half * 8 + (k + d) % 8] for d in range(1, 8)]
+    roots = [cores[ROOT_K], cores[8 + ROOT_K]]
+    is_root = core in roots
+
+    def did(c):
+        rid, pid, _se = topo.addr(c)
+        return DstId(rid=rid, pnc=pid)
+
+    def blk(r):
+        return T.land[:, 128 * r:128 * (r + 1)]
+
+    sent = 0
+
+    g.scalar.dma_start(T.g1[rank], T.x1[:]).then_inc(S.ld1, 16)
+    g.sync.dma_start(blk(rank), T.x2[:]).then_inc(S.ld2, 16)
+
+    g.wait_ge(S.ld1, 16)
+    rd = [c for c in roots if c != core]
+    g.remote_dma_fused([RemoteDMATransfer(dst_ids=[did(c) for c in rd], dma_engine_mask=0x00FF, remote_sem=S.a1,
+                                          srcs=[T.g1[rank]], dsts=[T.g1[rank] for _c in rd], alu_op=0)],
+                       local_sem=S.sent)
+    sent += 8
+
+    g.wait_ge(S.ld2, 16)
+    rid, pid, _se = topo.addr(partner)
+    g.remote_dma(blk(rank), blk(rank), S.xarr, S.sent, pid, rid, 0x00FF)
+    sent += 8
+    g.remote_dma_fused([
+        RemoteDMATransfer(dst_ids=[did(c) for c in peers[:3]], dma_engine_mask=0x00FF, remote_sem=S.arrA,
+                          srcs=[blk(rank)], dsts=[blk(rank)] * 3, alu_op=0),
+        RemoteDMATransfer(dst_ids=[did(c) for c in peers[3:]], dma_engine_mask=0xFF00, remote_sem=S.arrA,
+                          srcs=[blk(rank)], dsts=[blk(rank)] * 4, alu_op=0),
+    ], local_sem=S.sent)
+    sent += 16
+
+    if is_root:
+        g.wait_ge(S.a1, 15 * 8)
+        fd = peers + [c for c in roots if c != core]
+        g.remote_dma_fused([RemoteDMATransfer(dst_ids=[did(c) for c in fd], dma_engine_mask=0x00FF, remote_sem=S.r1,
+                                              srcs=[T.g1[j] for j in range(16)], dsts=[T.res[:]] * len(fd),
+                                              alu_op=1)],
+                           local_sem=S.sent)
+        sent += 8
+
+    g.wait_ge(S.xarr, 8)
+    g.remote_dma_fused([RemoteDMATransfer(dst_ids=[did(c) for c in peers], dma_engine_mask=0xFFFF, remote_sem=S.arrB,
+                                          srcs=[blk(partner_rank)], dsts=[blk(partner_rank)] * 7, alu_op=0)],
+                       local_sem=S.sent)
+    sent += 16
+
+    own = slice(1024 * half, 1024 * (half + 1))
+    oth = slice(1024 * (1 - half), 1024 * (2 - half))
+    g.sync.wait_ge(S.ld2, 16)
+    g.sync.wait_ge(S.arrA, 7 * 8)
+    g.sync.dma_start(T.y2[:, own], T.land[:, own]).then_inc(S.st1, 16)
+    g.sync.wait_ge(S.r1, 8)
+    g.sync.dma_start(T.y1[:], T.res[:]).then_inc(S.sty, 16)
+
+    g.scalar.wait_ge(S.xarr, 8)
+    g.scalar.wait_ge(S.arrB, 7 * 16)
+    g.scalar.dma_start(T.y2[:, oth], T.land[:, oth]).then_inc(S.st2, 16)
+
+    g.wait_ge(S.sent, sent)
+    g.wait_ge(S.st1, 16)
+    g.wait_ge(S.sty, 16)
+    g.wait_ge(S.st2, 16)

@@ -5,69 +5,81 @@ SCRATCH = {
     "g1": ("dram", [16, 128, 16], "float32"),
     "res": ("dram", [128, 16], "float32"),
 }
-SEMAPHORES = ["ld1", "ld2", "xarr", "arrA", "arrB", "a1", "r1", "sent", "st1", "st2", "sty"]
+SEMAPHORES = ["ld1", "ld2", "xarr", "arrA", "arrB", "a1", "p1", "r1", "sent", "st1", "st2", "sty"]
 
-ROOT_K = 0
+ROOT_K = 2
 
 
 def rank_program(g, core, T, topo):
-    rank = T.rank_of(core)
-    if rank is None:
-        return
     S = T.sem
     cores = T.cores
-    half, k = divmod(rank, 8)
-    partner_rank = (1 - half) * 8 + k
-    partner = cores[partner_rank]
-    peers = [cores[half * 8 + (k + d) % 8] for d in range(1, 8)]
-    roots = [cores[ROOT_K], cores[8 + ROOT_K]]
-    is_root = core in roots
 
     def did(c):
         rid, pid, _se = topo.addr(c)
         return DstId(rid=rid, pnc=pid)
 
+    helpers = [(topo.chip(cores[8 * h]) ^ 1) * 8 + ROOT_K for h in range(2)]
+    if core in helpers:
+        h = helpers.index(core)
+        g.wait_ge(S.p1, 2 * 8)
+        g.remote_dma_fused([RemoteDMATransfer(dst_ids=[did(c) for c in cores[8 * h:8 * h + 8]],
+                                              dma_engine_mask=0x00FF, remote_sem=S.r1,
+                                              srcs=[T.g1[0], T.g1[1]], dsts=[T.res[:]] * 8, alu_op=1)],
+                           local_sem=S.sent)
+        g.wait_ge(S.sent, 8)
+        return
+
+    rank = T.rank_of(core)
+    if rank is None:
+        return
+    half, k = divmod(rank, 8)
+    partner_rank = (1 - half) * 8 + k
+    partner = cores[partner_rank]
+    peers = [cores[half * 8 + (k + d) % 8] for d in range(1, 8)]
+    root = cores[half * 8 + ROOT_K]
+    sent = [0]
+
     def blk(r):
         return T.land[:, 128 * r:128 * (r + 1)]
-
-    sent = 0
 
     g.scalar.dma_start(T.g1[rank], T.x1[:]).then_inc(S.ld1, 16)
     g.sync.dma_start(blk(rank), T.x2[:]).then_inc(S.ld2, 16)
 
-    g.wait_ge(S.ld1, 16)
-    rd = [c for c in roots if c != core]
-    g.remote_dma_fused([RemoteDMATransfer(dst_ids=[did(c) for c in rd], dma_engine_mask=0x00FF, remote_sem=S.a1,
-                                          srcs=[T.g1[rank]], dsts=[T.g1[rank] for _c in rd], alu_op=0)],
-                       local_sem=S.sent)
-    sent += 8
+    if core != root:
+        g.wait_ge(S.ld1, 16)
+        g.remote_dma_fused([RemoteDMATransfer(dst_ids=[did(root)], dma_engine_mask=0xFF00, remote_sem=S.a1,
+                                              srcs=[T.g1[rank]], dsts=[T.g1[rank]], alu_op=0)],
+                           local_sem=S.sent)
+        sent[0] += 8
 
     g.wait_ge(S.ld2, 16)
     rid, pid, _se = topo.addr(partner)
     g.remote_dma(blk(rank), blk(rank), S.xarr, S.sent, pid, rid, 0x00FF)
-    sent += 8
+    sent[0] += 8
     g.remote_dma_fused([
         RemoteDMATransfer(dst_ids=[did(c) for c in peers[:3]], dma_engine_mask=0x00FF, remote_sem=S.arrA,
                           srcs=[blk(rank)], dsts=[blk(rank)] * 3, alu_op=0),
         RemoteDMATransfer(dst_ids=[did(c) for c in peers[3:]], dma_engine_mask=0xFF00, remote_sem=S.arrA,
                           srcs=[blk(rank)], dsts=[blk(rank)] * 4, alu_op=0),
     ], local_sem=S.sent)
-    sent += 16
+    sent[0] += 16
 
-    if is_root:
-        g.wait_ge(S.a1, 15 * 8)
-        fd = peers + [c for c in roots if c != core]
-        g.remote_dma_fused([RemoteDMATransfer(dst_ids=[did(c) for c in fd], dma_engine_mask=0x00FF, remote_sem=S.r1,
-                                              srcs=[T.g1[j] for j in range(16)], dsts=[T.res[:]] * len(fd),
-                                              alu_op=1)],
+    if core == root:
+        g.wait_ge(S.ld1, 16)
+        g.wait_ge(S.a1, 7 * 8)
+        g.remote_dma_fused([RemoteDMATransfer(dst_ids=[did(c) for c in helpers], dma_engine_mask=0x00FF,
+                                              remote_sem=S.p1,
+                                              srcs=[T.g1[half * 8 + j] for j in range(8)],
+                                              dsts=[T.g1[half]] * 2, alu_op=1)],
                            local_sem=S.sent)
-        sent += 8
+        sent[0] += 8
 
     g.wait_ge(S.xarr, 8)
-    g.remote_dma_fused([RemoteDMATransfer(dst_ids=[did(c) for c in peers], dma_engine_mask=0xFFFF, remote_sem=S.arrB,
-                                          srcs=[blk(partner_rank)], dsts=[blk(partner_rank)] * 7, alu_op=0)],
+    g.remote_dma_fused([RemoteDMATransfer(dst_ids=[did(c) for c in peers], dma_engine_mask=0xFFFF,
+                                          remote_sem=S.arrB, srcs=[blk(partner_rank)],
+                                          dsts=[blk(partner_rank)] * 7, alu_op=0)],
                        local_sem=S.sent)
-    sent += 16
+    sent[0] += 16
 
     own = slice(1024 * half, 1024 * (half + 1))
     oth = slice(1024 * (1 - half), 1024 * (2 - half))
@@ -81,7 +93,7 @@ def rank_program(g, core, T, topo):
     g.scalar.wait_ge(S.arrB, 7 * 16)
     g.scalar.dma_start(T.y2[:, oth], T.land[:, oth]).then_inc(S.st2, 16)
 
-    g.wait_ge(S.sent, sent)
+    g.wait_ge(S.sent, sent[0])
     g.wait_ge(S.st1, 16)
     g.wait_ge(S.sty, 16)
     g.wait_ge(S.st2, 16)

from concourse.bass import DstId, RemoteDMATransfer

SCRATCH = {
    "land": ("sbuf", [128, 2048], "float32"),
    "g1": ("dram", [16, 128, 16], "float32"),
    "res": ("dram", [128, 16], "float32"),
}
SEMAPHORES = ["ld1", "ld2", "xarr", "arrA", "arrB", "a1", "p1", "r1", "sent", "st1", "st2", "sty"]

ROOT_K = 2


def rank_program(g, core, T, topo):
    S = T.sem
    cores = T.cores

    def did(c):
        rid, pid, _se = topo.addr(c)
        return DstId(rid=rid, pnc=pid)

    helpers = [(topo.chip(cores[8 * h]) ^ 1) * 8 + ROOT_K for h in range(2)]
    if core in helpers:
        h = helpers.index(core)
        g.wait_ge(S.p1, 2 * 8)
        g.remote_dma_fused([RemoteDMATransfer(dst_ids=[did(c) for c in cores[8 * h:8 * h + 8]],
                                              dma_engine_mask=0x00FF, remote_sem=S.r1,
                                              srcs=[T.g1[0], T.g1[1]], dsts=[T.res[:]] * 8, alu_op=1)],
                           local_sem=S.sent)
        g.wait_ge(S.sent, 8)
        return

    rank = T.rank_of(core)
    if rank is None:
        return
    half, k = divmod(rank, 8)
    partner_rank = (1 - half) * 8 + k
    partner = cores[partner_rank]
    peers = [cores[half * 8 + (k + d) % 8] for d in range(1, 8)]
    root = cores[half * 8 + ROOT_K]
    sent = [0]

    def blk(r):
        return T.land[:, 128 * r:128 * (r + 1)]

    g.scalar.dma_start(T.g1[rank], T.x1[:]).then_inc(S.ld1, 16)
    g.sync.dma_start(blk(rank), T.x2[:]).then_inc(S.ld2, 16)

    if core != root:
        g.wait_ge(S.ld1, 16)
        g.remote_dma_fused([RemoteDMATransfer(dst_ids=[did(root)], dma_engine_mask=0xFF00, remote_sem=S.a1,
                                              srcs=[T.g1[rank]], dsts=[T.g1[rank]], alu_op=0)],
                           local_sem=S.sent)
        sent[0] += 8

    g.wait_ge(S.ld2, 16)
    rid, pid, _se = topo.addr(partner)
    g.remote_dma(blk(rank), blk(rank), S.xarr, S.sent, pid, rid, 0x00FF)
    sent[0] += 8
    g.remote_dma_fused([
        RemoteDMATransfer(dst_ids=[did(c) for c in peers[:3]], dma_engine_mask=0x00FF, remote_sem=S.arrA,
                          srcs=[blk(rank)], dsts=[blk(rank)] * 3, alu_op=0),
        RemoteDMATransfer(dst_ids=[did(c) for c in peers[3:]], dma_engine_mask=0xFF00, remote_sem=S.arrA,
                          srcs=[blk(rank)], dsts=[blk(rank)] * 4, alu_op=0),
    ], local_sem=S.sent)
    sent[0] += 16

    if core == root:
        g.wait_ge(S.ld1, 16)
        g.wait_ge(S.a1, 7 * 8)
        g.remote_dma_fused([RemoteDMATransfer(dst_ids=[did(c) for c in helpers], dma_engine_mask=0x00FF,
                                              remote_sem=S.p1,
                                              srcs=[T.g1[half * 8 + j] for j in range(8)],
                                              dsts=[T.g1[half]] * 2, alu_op=1)],
                           local_sem=S.sent)
        sent[0] += 8

    g.wait_ge(S.xarr, 8)
    g.remote_dma_fused([RemoteDMATransfer(dst_ids=[did(c) for c in peers], dma_engine_mask=0xFFFF,
                                          remote_sem=S.arrB, srcs=[blk(partner_rank)],
                                          dsts=[blk(partner_rank)] * 7, alu_op=0)],
                       local_sem=S.sent)
    sent[0] += 16

    own = slice(1024 * half, 1024 * (half + 1))
    oth = slice(1024 * (1 - half), 1024 * (2 - half))
    g.sync.wait_ge(S.ld2, 16)
    g.sync.wait_ge(S.arrA, 7 * 8)
    g.sync.dma_start(T.y2[:, own], T.land[:, own]).then_inc(S.st1, 16)
    g.sync.wait_ge(S.r1, 8)
    g.sync.dma_start(T.y1[:], T.res[:]).then_inc(S.sty, 16)

    g.scalar.wait_ge(S.xarr, 8)
    g.scalar.wait_ge(S.arrB, 7 * 16)
    g.scalar.dma_start(T.y2[:, oth], T.land[:, oth]).then_inc(S.st2, 16)

    g.wait_ge(S.sent, sent[0])
    g.wait_ge(S.st1, 16)
    g.wait_ge(S.sty, 16)
    g.wait_ge(S.st2, 16)
